import numpy as np
import ml_dtypes


def mxq(x, axis, fmt="e4m3"):
    dtype, down = {"e4m3": (ml_dtypes.float8_e4m3fn, 7), "e5m2": (ml_dtypes.float8_e5m2, 14)}[fmt]
    v = np.moveaxis(np.asarray(x, np.float32).astype(ml_dtypes.bfloat16).astype(np.float64), axis, -1)
    blocks = v.reshape(v.shape[:-1] + (-1, 32))
    amax = np.abs(blocks).max(-1, keepdims=True)
    byte = np.maximum(np.where(amax > 0, np.frexp(amax)[1] - 1 + 127, 0) - down, 1)
    scale = np.exp2(byte - 127.0)
    codes = (blocks / scale).astype(np.float32).astype(dtype).astype(np.float64)
    return np.moveaxis((codes * scale).reshape(v.shape), -1, axis)


WIDE = False


def mx_kscale(k):
    if not WIDE:
        return np.ones(k)
    levels = np.array([10, -10, 5, -5, 0])
    if k % 512:
        return np.exp2(np.random.permutation(np.resize(levels, k // 32))).repeat(32)
    a = np.empty((k // 512, 16))
    for p in range(k // 512):
        a[p, :8] = np.random.permutation(np.resize(levels, 8))
        for g in range(8):
            far = levels[np.abs(levels - a[p, g]) >= 10]
            a[p, g + 8] = far[np.random.randint(len(far))]
    return np.exp2(a.ravel()).repeat(32)


BF16 = ml_dtypes.bfloat16


def bf(x):
    return np.asarray(x, np.float32).astype(BF16)


def f64(x):
    return np.asarray(x).astype(np.float64)


E2M1 = np.array([0.0, 0.5, 1.0, 1.5, 2.0, 3.0, 4.0, 6.0, -0.0, -0.5, -1.0, -1.5, -2.0, -3.0, -4.0, -6.0])


def pack_weight(w, fmt):
    k, n = w.shape
    w = f64(bf(w)).reshape(k // 32, 32, n)
    amax = np.abs(w).max(1)
    if fmt == "e4m3":
        byte = np.frexp(amax)[1] - 1 + 127 - 7
    else:
        mant, ex = np.frexp(amax / 6.0)
        byte = np.where(mant > 0.5, ex, ex - 1) + 127
    byte = np.clip(np.where(amax > 0, byte, 1), 1, 254)
    scaled = (w * np.exp2(127.0 - byte)[:, None, :]).reshape(k, n).astype(np.float32)
    by_word = np.ascontiguousarray(scaled.reshape(k // 512, 128, 4, n).transpose(0, 1, 3, 2))
    if fmt == "e4m3":
        words = by_word.astype(ml_dtypes.float8_e4m3fn).view(np.uint8)
    else:
        c = by_word.astype(ml_dtypes.float4_e2m1fn).view(np.uint8) & 0xF
        words = c[..., 0::2] | (c[..., 1::2] << 4)
    return np.ascontiguousarray(words), np.ascontiguousarray(byte.astype(np.uint8).reshape(k // 512, 16, n))


def unpack_weight(words, scales, fmt):
    g, p, n, _ = words.shape
    if fmt == "e4m3":
        vals = np.ascontiguousarray(words).view(ml_dtypes.float8_e4m3fn).astype(np.float64)
    else:
        nib = np.empty((g, p, n, 4), np.uint8)
        nib[..., 0::2] = words & 0xF
        nib[..., 1::2] = words >> 4
        vals = E2M1[nib]
    vals = vals * np.repeat(np.exp2(scales.astype(np.float64) - 127.0), 8, axis=1)[..., None]
    return vals.transpose(0, 1, 3, 2).reshape(g * 512, n)
def pack4(w):
    words, scales = pack_weight(w, "e2m1")
    return words.reshape(words.shape[0], 128, -1), scales


def unpack4(words, scales):
    return unpack_weight(words.reshape(words.shape[0], 128, -1, 2), scales, "e2m1")


def planes(Y):
    n, m = Y.shape
    b = f64(bf(Y)).reshape(n // 32, 32, m)
    amax = np.abs(b).max(1)
    byte = np.clip(np.where(amax > 0, np.frexp(amax)[1] - 1 + 127 - 7, 1), 1, 254)
    codes = (b * np.exp2(127.0 - byte)[:, None, :]).reshape(n, m).astype(np.float32).astype(ml_dtypes.float8_e4m3fn).view(np.uint8)
    words = codes.reshape(n // 512, 128, 4, m).transpose(0, 1, 3, 2)
    return np.ascontiguousarray(words), np.ascontiguousarray(byte.astype(np.uint8).reshape(n // 512, 16, m))


M, D, H, E = 768, 1536, 2048, 1024

BIAS = 0.3
DIM_SPREAD = 0.8
IMAGE_SPREAD = 0.3


def setup_inputs():
    s = mx_kscale(D)
    t = mx_kscale(H)
    pooled = np.random.randn(M, D) * s
    w_hidden = np.random.randn(D, H) / np.sqrt(D) / s[:, None] * t
    b_hidden = BIAS * np.random.randn(H) * t
    w_proj = np.random.randn(H, E) * np.sqrt(2.0 / H) / t[:, None]
    b_proj = BIAS * np.random.randn(E)
    hidden_words, hidden_scales = pack4(w_hidden)
    proj_words, proj_scales = pack4(w_proj)
    return {"pooled": bf(pooled),
            "hidden_words": hidden_words, "hidden_scales": hidden_scales, "b_hidden": bf(b_hidden),
            "proj_words": proj_words, "proj_scales": proj_scales, "b_proj": bf(b_proj),
            "dim_weight": bf(np.exp(DIM_SPREAD * np.random.randn(E))),
            "image_weight": bf(np.exp(IMAGE_SPREAD * np.random.randn(M)))}


def reference(pooled, hidden_words, hidden_scales, b_hidden, proj_words, proj_scales, b_proj, dim_weight, image_weight):
    w_hidden = unpack4(hidden_words, hidden_scales)
    w_proj = unpack4(proj_words, proj_scales)
    x = mxq(f64(pooled), 1, "e4m3")
    a = np.maximum((x @ w_hidden) + f64(b_hidden), 0.0)
    r = mxq(a, 1, "e4m3")
    z = (r @ w_proj) + f64(b_proj)
    y = z * f64(dim_weight) * f64(image_weight)[:, None]
    Y = y.T
    words, scales = planes(Y)
    return y, words, scales

@@ -1,0 +1,338 @@
+from contextlib import ExitStack
+
+import concourse.mybir as mybir
+from concourse.masks import make_identity
+
+M, D, H, E = 768, 1536, 2048, 1024
+FLOPS = 2 * M * (D * H + H * E)
+
+F32 = mybir.dt.float32
+BF16 = mybir.dt.bfloat16
+I32 = mybir.dt.int32
+U32 = mybir.dt.uint32
+U8 = mybir.dt.uint8
+FP8X4 = mybir.dt.float8_e4m3fn_x4
+FP4X4 = mybir.dt.float4_e2m1fn_x4
+ALU = mybir.AluOpType
+ACT = mybir.ActivationFunctionType
+
+P = 128
+G = 512
+TILES = M // P
+D_GROUPS, H_GROUPS, E_GROUPS = D // G, H // G, E // G
+BANKS = 8
+
+
+def tile_image_projection_for_similarity_h1_kernel(
+    tc, pooled, hidden_words, hidden_scales, b_hidden, proj_words, proj_scales, b_proj, dim_weight, image_weight,
+    out_0, out_1, out_2,
+):
+    nc = tc.nc
+    with ExitStack() as ctx:
+        keep = ctx.enter_context(tc.tile_pool(name="keep", bufs=1))
+        work = ctx.enter_context(tc.tile_pool(name="work", bufs=4))
+        psum = ctx.enter_context(tc.psum_pool(name="psum", bufs=1))
+        ctx.enter_context(tc.manual_schedule())
+
+        banks_taken = []
+
+        def next_bank():
+            n = len(banks_taken) % BANKS
+            banks_taken.append(n)
+            return psum.tile([P, G], F32, name="bank%d" % n)
+
+        def kept(name, shape, dtype):
+            return keep.tile(shape, dtype, name=name, align_bytes=64)
+
+        ident = kept("ident", [P, P], F32)
+        x_rows = [kept("x_rows%d" % i, [P, D], BF16) for i in range(TILES)]
+        wh = [kept("wh%d" % c, [P, D_GROUPS, 2 * G], U8) for c in range(H_GROUPS)]
+        wp = [kept("wp%d" % e, [P, H_GROUPS, 2 * G], U8) for e in range(E_GROUPS)]
+        wh_scale_first = kept("wh_scale_first", [P, D_GROUPS, G], U8)
+        wh_scale_rest = kept("wh_scale_rest", [P, D_GROUPS, H - G], U8)
+        wp_scale = kept("wp_scale", [P, H_GROUPS, E], U8)
+        bh_cols = kept("bh_cols", [P, H // P], BF16)
+        bp_cols = kept("bp_cols", [P, E // P], BF16)
+        dw_cols = kept("dw_cols", [P, E // P], BF16)
+        iw_rows = kept("iw_rows", [P, P], BF16)
+        iw_rows32 = kept("iw_rows32", [P, P], F32)
+        bh_all = kept("bh_all", [P, H], BF16)
+        bp_all = kept("bp_all", [P, E], BF16)
+        dw_all = kept("dw_all", [P, E], BF16)
+        iw_col = kept("iw_col", [P, TILES], F32)
+        y_scales = kept("y_scales", [P, E_GROUPS, M], U8)
+
+        nc.vector.memset(wh_scale_first[:].bitcast(I32), 0)
+        nc.vector.memset(wh_scale_rest[:].bitcast(I32), 0)
+        make_identity(nc, ident[:])
+        nc.gpsimd.memset(iw_rows[:], 0.0)
+        nc.gpsimd.memset(wp_scale[:].bitcast(I32), 0)
+
+        def load_x(i):
+            nc.sync.dma_start(out=x_rows[i][:], in_=pooled[i * P : (i + 1) * P, :])
+
+        def load_words(tile, words, c):
+            src = words.bitcast(I32)[:, :, c * G // 2 : (c + 1) * G // 2]
+            nc.sync.dma_start(out=tile[:].bitcast(I32), in_=src.rearrange("g p w -> p g w"))
+
+        def load_scales(tile, scales, first, last):
+            for q in range(4):
+                src = scales.bitcast(I32)[:, 4 * q : 4 * q + 4, first // 4 : last // 4]
+                nc.sync.dma_start(out=tile[32 * q : 32 * q + 4].bitcast(I32), in_=src.rearrange("g r w -> r g w"))
+
+        def load_cols(tile, vec):
+            nc.sync.dma_start(out=tile[:], in_=vec.rearrange("(p c) -> p c", p=P))
+
+        load_cols(bh_cols, b_hidden)
+        load_x(0)
+        load_scales(wh_scale_first, hidden_scales, 0, G)
+        load_words(wh[0], hidden_words, 0)
+        load_words(wh[1], hidden_words, 1)
+        load_scales(wh_scale_rest, hidden_scales, G, H)
+        load_x(1)
+        load_words(wh[2], hidden_words, 2)
+        load_words(wh[3], hidden_words, 3)
+        load_cols(bp_cols, b_proj)
+        load_cols(dw_cols, dim_weight)
+        nc.sync.dma_start(out=iw_rows[0:TILES, :], in_=image_weight.rearrange("(i m) -> i m", m=P))
+        load_x(2)
+        load_scales(wp_scale, proj_scales, 0, E)
+        load_words(wp[0], proj_words, 0)
+        load_words(wp[1], proj_words, 1)
+        for i in range(3, TILES):
+            load_x(i)
+
+        def spread(cols, picks):
+            bank = next_bank()
+            words = cols[:].bitcast(F32)
+            for slot, c in enumerate(picks):
+                nc.tensor.transpose(
+                    bank[:, slot * P : (slot + 1) * P], words[:, c : c + 1].to_broadcast([P, P]), ident[:]
+                )
+            return bank
+
+        x_codes, x_scales, a_rows, a_codes, a_scales = {}, {}, {}, {}, {}
+        z_biased, y_full, y_rows, a_banks, a_cols = {}, {}, {}, {}, {}
+
+        def turn(halves):
+            bank = next_bank()
+            for slot, half in enumerate(halves):
+                nc.tensor.transpose(bank[:, slot * P : (slot + 1) * P], half, ident[:])
+            return bank
+
+        def x_halves(i, groups):
+            words = x_rows[i][:].bitcast(F32)
+            return [words[:, 256 * g + u : 256 * (g + 1) : 2] for g in groups for u in range(2)]
+
+        def sorted_halves(tiles):
+            return [t[:].bitcast(F32)[:, u * P : (u + 1) * P] for t in tiles for u in range(2)]
+
+        def join_halves(bank, count):
+            cols = work.tile([P, 2 * G], BF16, name="cols", align_bytes=64)
+            nc.scalar.copy(
+                out=cols[:, 0 : count * G].bitcast(F32).rearrange("p (g m u) -> p g m u", g=count, u=2),
+                in_=bank[:, 0 : count * 2 * P].rearrange("p (g u m) -> p g m u", g=count, u=2),
+            )
+            return cols
+
+        def turn_x(i, runs):
+            return [(groups, turn(x_halves(i, groups))) for groups in runs]
+
+        def quantize_x(i, turned):
+            x_codes[i] = work.tile([P, D_GROUPS, P], U32, name="x_codes", bufs=2, align_bytes=64)
+            x_scales[i] = work.tile([P, D_GROUPS, P], U8, name="x_scales", bufs=2, align_bytes=64)
+            for groups, bank in turned:
+                cols = join_halves(bank, len(groups))
+                for slot, g in enumerate(groups):
+                    nc.vector.quantize_mx(
+                        out=x_codes[i][:, g, :].bitcast(FP8X4),
+                        scales=x_scales[i][:, g, :],
+                        in_=cols[:, slot * G : (slot + 1) * G],
+                    )
+
+        def hidden(i, c):
+            bank = next_bank()
+            for g in range(D_GROUPS):
+                if c == 0:
+                    w_scale = wh_scale_first[:, g, :]
+                else:
+                    w_scale = wh_scale_rest[:, g, (c - 1) * G : c * G]
+                nc.tensor.matmul_mx(
+                    out=bank[:],
+                    lhsT=x_codes[i][:, g, :].bitcast(FP8X4),
+                    lhsT_scale=x_scales[i][:, g, :],
+                    rhs=wh[c][:, g, :].bitcast(FP4X4),
+                    rhs_scale=w_scale,
+                    start=(g == 0),
+                    stop=(g == D_GROUPS - 1),
+                )
+            a_rows[i, c] = work.tile([P, G], BF16, name="a_rows", bufs=8, align_bytes=64)
+            nc.vector.tensor_tensor(
+                out=a_rows[i, c][:].rearrange("m (u q j) -> m u q j", u=2, j=2),
+                in0=bank[:].rearrange("m (q u j) -> m u q j", u=2, j=2),
+                in1=bh_all[:, c * G : (c + 1) * G].rearrange("m (u q j) -> m u q j", u=2, j=2),
+                op=ALU.add,
+            )
+
+        def turn_a(i):
+            for pair in range(H_GROUPS // 2):
+                a_banks[i, pair] = turn(sorted_halves([a_rows[i, 2 * pair], a_rows[i, 2 * pair + 1]]))
+
+        def relu_a(i):
+            for g in range(H_GROUPS):
+                a_cols[i, g] = work.tile([P, G], BF16, name="a_cols", bufs=8, align_bytes=64)
+                pairs = a_banks[i, g // 2][:].bitcast(BF16)[:, (g % 2) * G : (g % 2 + 1) * G]
+                nc.scalar.activation(
+                    out=a_cols[i, g][:].rearrange("p (m u j) -> p m u j", u=2, j=2),
+                    in_=pairs.rearrange("p (u m j) -> p m u j", u=2, j=2),
+                    func=ACT.Relu,
+                )
+
+        def quantize_a(i, g):
+            a_codes[i, g] = work.tile([P, P], U32, name="a_codes", bufs=8, align_bytes=64)
+            a_scales[i, g] = work.tile([P, P], U8, name="a_scales", bufs=8, align_bytes=64)
+            nc.vector.quantize_mx(out=a_codes[i, g][:].bitcast(FP8X4), scales=a_scales[i, g][:], in_=a_cols[i, g][:])
+
+        def project(i, e, first=0, width=G):
+            bank = next_bank()
+            for g in range(H_GROUPS):
+                nc.tensor.matmul_mx(
+                    out=bank[:, 0:width],
+                    lhsT=a_codes[i, g][:].bitcast(FP8X4),
+                    lhsT_scale=a_scales[i, g][:],
+                    rhs=wp[e][:, g, 2 * first : 2 * (first + width)].bitcast(FP4X4),
+                    rhs_scale=wp_scale[:, g, e * G + first : e * G + first + width],
+                    start=(g == 0),
+                    stop=(g == H_GROUPS - 1),
+                )
+            return bank
+
+        def add_proj_bias(i, e, bank, first=0, width=G):
+            if first == 0:
+                z_biased[i, e] = work.tile([P, G], F32, name="z_biased")
+            nc.vector.tensor_tensor(
+                out=z_biased[i, e][:, first : first + width],
+                in0=bank[:, 0:width],
+                in1=bp_all[:, e * G + first : e * G + first + width],
+                op=ALU.add,
+            )
+
+        def weigh(i, e, first=0, width=G):
+            if first == 0:
+                y_full[i, e] = work.tile([P, G], F32, name="y", bufs=6)
+                y_rows[i, e] = work.tile([P, G], BF16, name="y_rows", bufs=6, align_bytes=64)
+            y = y_full[i, e][:, first : first + width]
+            nc.vector.scalar_tensor_tensor(
+                out=y,
+                in0=z_biased[i, e][:, first : first + width],
+                scalar=iw_col[:, i : i + 1],
+                in1=dw_all[:, e * G + first : e * G + first + width],
+                op0=ALU.mult,
+                op1=ALU.mult,
+            )
+            if first + width == G:
+                nc.sync.dma_start(out=out_0[i * P : (i + 1) * P, e * G : (e + 1) * G], in_=y_full[i, e][:])
+            nc.scalar.copy(
+                out=y_rows[i, e][:].rearrange("m (u q j) -> m u q j", u=2, j=2)[:, :, first // 4 : (first + width) // 4, :],
+                in_=y.rearrange("m (q u j) -> m u q j", u=2, j=2),
+            )
+
+        def turn_y(i, groups):
+            return turn(sorted_halves([y_rows[i, e] for e in groups]))
+
+        out_words = out_1.rearrange("g p m t -> g p (m t)").bitcast(I32)
+
+        def quantize_y(i, groups, cols):
+            for slot, e in enumerate(groups):
+                codes = work.tile([P, P], U32, name="y_codes", bufs=6, align_bytes=64)
+                nc.vector.quantize_mx(
+                    out=codes[:].bitcast(FP8X4),
+                    scales=y_scales[:, e, i * P : (i + 1) * P],
+                    in_=cols[:, slot * G : (slot + 1) * G],
+                )
+                nc.sync.dma_start(out=out_words[e, :, i * P : (i + 1) * P], in_=codes[:].bitcast(I32))
+
+        for u in range(2):
+            bank = spread(bh_cols, [2 * a + u for a in range(4)])
+            nc.vector.tensor_copy(
+                out=bh_all[:].bitcast(F32).rearrange("p (c u jj a) -> p u c jj a", c=H_GROUPS, u=2, a=4)[:, u],
+                in_=bank[:].rearrange("p (a c jj) -> p c jj a", a=4, c=H_GROUPS),
+            )
+        quantize_x(0, turn_x(0, [[g] for g in range(D_GROUPS)]))
+
+        both = list(range(E_GROUPS))
+        last = TILES - 1
+        for i in range(TILES):
+            if i == last:
+                early_bank = project(i - 1, 0)
+                weigh(i - 2, 1)
+                add_proj_bias(i - 1, 0, early_bank)
+            for c in range(H_GROUPS):
+                hidden(i, c)
+                if c == 0 and i >= 2:
+                    if i == last:
+                        weigh(i - 1, 0)
+                    else:
+                        weigh(i - 2, 1)
+                if c == 1 and i == 0:
+                    quantize_x(1, turn_x(1, [[0, 1], [2]]))
+            if i == 0:
+                nc.vector.tensor_copy(out=iw_rows32[:], in_=iw_rows[:])
+                spread_banks = [spread(cols, range(4)) for cols in (bp_cols, dw_cols)]
+                iw_bank = turn([iw_rows32[:]])
+                turn_a(i)
+                relu_a(i)
+                for bank, dst in zip(spread_banks, (bp_all, dw_all)):
+                    nc.scalar.copy(
+                        out=dst[:].bitcast(F32).rearrange("p (j c) -> p j c", c=4),
+                        in_=bank[:].rearrange("p (c j) -> p j c", c=4),
+                    )
+                nc.scalar.copy(out=iw_col[:], in_=iw_bank[:, 0:TILES])
+                for g in range(H_GROUPS):
+                    quantize_a(i, g)
+                continue
+            x_turned = turn_x(i + 1, [[0, 1], [2]]) if i < last else []
+            y_bank = turn_y(i - 2, both) if i >= 2 else None
+            turn_a(i)
+            if i < last:
+                quantize_x(i + 1, x_turned)
+            relu_a(i)
+            y_cols = join_halves(y_bank, E_GROUPS) if i >= 2 else None
+            quantize_a(i, 0)
+            if i < last:
+                add_proj_bias(i - 1, 0, project(i - 1, 0))
+                quantize_a(i, 1)
+                weigh(i - 1, 0)
+                quantize_a(i, 2)
+                quantize_a(i, 3)
+                if i >= 2:
+                    quantize_y(i - 2, both, y_cols)
+                add_proj_bias(i - 1, 1, project(i - 1, 1))
+
+        quantize_a(last, 1)
+        add_proj_bias(last - 1, 1, project(last - 1, 1))
+        quantize_a(last, 2)
+        quantize_a(last, 3)
+        bank0 = project(last, 0)
+        weigh(last - 1, 1)
+        add_proj_bias(last, 0, bank0)
+        part_banks = [project(last, 1, first, P) for first in range(0, G, P)]
+        quantize_y(last - 2, both, y_cols)
+        weigh(last, 0)
+        before_cols = join_halves(turn_y(last - 1, both), E_GROUPS)
+        for part, bank in enumerate(part_banks):
+            add_proj_bias(last, 1, bank, part * P, P)
+            if part > 0:
+                weigh(last, 1, (part - 1) * P, P)
+        first_cols = join_halves(turn_y(last, [0]), 1)
+        quantize_y(last - 1, [0], before_cols)
+        weigh(last, 1, G - P, P)
+        quantize_y(last - 1, [1], before_cols[:, G : 2 * G])
+        quantize_y(last, [0], first_cols)
+        quantize_y(last, [1], join_halves(turn_y(last, [1]), 1))
+        for q in range(4):
+            queue = nc.scalar if q % 2 == 0 else nc.sync
+            queue.dma_start(
+                out=out_2.bitcast(I32)[:, 4 * q : 4 * q + 4, :].rearrange("g r w -> r g w"),
+                in_=y_scales[32 * q : 32 * q + 4].bitcast(I32),
+            )

@@ -42,14 +42,14 @@ def tile_image_projection_for_similarity_h1_kernel(
             return psum.tile([P, G], F32, name="bank%d" % n)
 
         def kept(name, shape, dtype):
-            return keep.tile(shape, dtype, name=name, align_bytes=64)
+            return keep.tile(shape, dtype, name=name, align_bytes=256)
 
         ident = kept("ident", [P, P], F32)
         x_rows = [kept("x_rows%d" % i, [P, D], BF16) for i in range(TILES)]
-        wh = [kept("wh%d" % c, [P, D_GROUPS, 2 * G], U8) for c in range(H_GROUPS)]
-        wp = [kept("wp%d" % e, [P, H_GROUPS, 2 * G], U8) for e in range(E_GROUPS)]
-        wh_scale_first = kept("wh_scale_first", [P, D_GROUPS, G], U8)
-        wh_scale_rest = kept("wh_scale_rest", [P, D_GROUPS, H - G], U8)
+        wh = [kept("wh%d" % g, [P, 2 * H], U8) for g in range(D_GROUPS)]
+        wp = [kept("wp%d" % half, [P, 2, 2 * E], U8) for half in range(H_GROUPS // 2)]
+        wh_scale_first = kept("wh_scale_first", [P, 1, H], U8)
+        wh_scale_rest = kept("wh_scale_rest", [P, D_GROUPS - 1, H], U8)
         wp_scale = kept("wp_scale", [P, H_GROUPS, E], U8)
         bh_cols = kept("bh_cols", [P, H // P], BF16)
         bp_cols = kept("bp_cols", [P, E // P], BF16)
@@ -65,19 +65,22 @@ def tile_image_projection_for_similarity_h1_kernel(
         nc.vector.memset(wh_scale_first[:].bitcast(I32), 0)
         nc.vector.memset(wh_scale_rest[:].bitcast(I32), 0)
         make_identity(nc, ident[:])
-        nc.gpsimd.memset(iw_rows[:], 0.0)
+        nc.scalar.activation(out=iw_rows[:], in_=ident[:], func=ACT.Copy, scale=0.0)
         nc.gpsimd.memset(wp_scale[:].bitcast(I32), 0)
 
         def load_x(i):
             nc.sync.dma_start(out=x_rows[i][:], in_=pooled[i * P : (i + 1) * P, :])
 
-        def load_words(tile, words, c):
-            src = words.bitcast(I32)[:, :, c * G // 2 : (c + 1) * G // 2]
-            nc.sync.dma_start(out=tile[:].bitcast(I32), in_=src.rearrange("g p w -> p g w"))
+        def load_wh(g):
+            nc.sync.dma_start(out=wh[g][:].bitcast(I32), in_=hidden_words.bitcast(I32)[g])
+
+        def load_wp(half):
+            src = proj_words.bitcast(I32)[2 * half : 2 * half + 2]
+            nc.sync.dma_start(out=wp[half][:].bitcast(I32), in_=src.rearrange("g p w -> p g w"))
 
         def load_scales(tile, scales, first, last):
             for q in range(4):
-                src = scales.bitcast(I32)[:, 4 * q : 4 * q + 4, first // 4 : last // 4]
+                src = scales.bitcast(I32)[first:last, 4 * q : 4 * q + 4, :]
                 nc.sync.dma_start(out=tile[32 * q : 32 * q + 4].bitcast(I32), in_=src.rearrange("g r w -> r g w"))
 
         def load_cols(tile, vec):
@@ -85,20 +88,19 @@ def tile_image_projection_for_similarity_h1_kernel(
 
         load_cols(bh_cols, b_hidden)
         load_x(0)
-        load_scales(wh_scale_first, hidden_scales, 0, G)
-        load_words(wh[0], hidden_words, 0)
-        load_words(wh[1], hidden_words, 1)
-        load_scales(wh_scale_rest, hidden_scales, G, H)
+        load_scales(wh_scale_first, hidden_scales, 0, 1)
+        load_wh(0)
+        load_scales(wh_scale_rest, hidden_scales, 1, D_GROUPS)
+        load_wh(1)
+        load_wh(2)
         load_x(1)
-        load_words(wh[2], hidden_words, 2)
-        load_words(wh[3], hidden_words, 3)
         load_cols(bp_cols, b_proj)
+        load_x(2)
         load_cols(dw_cols, dim_weight)
         nc.sync.dma_start(out=iw_rows[0:TILES, :], in_=image_weight.rearrange("(i m) -> i m", m=P))
-        load_x(2)
-        load_scales(wp_scale, proj_scales, 0, E)
-        load_words(wp[0], proj_words, 0)
-        load_words(wp[1], proj_words, 1)
+        load_scales(wp_scale, proj_scales, 0, H_GROUPS)
+        load_wp(0)
+        load_wp(1)
         for i in range(3, TILES):
             load_x(i)
 
@@ -111,7 +113,7 @@ def tile_image_projection_for_similarity_h1_kernel(
                 )
             return bank
 
-        x_codes, x_scales, a_rows, a_codes, a_scales = {}, {}, {}, {}, {}
+        x_sorted, x_codes, x_scales, a_rows, a_codes, a_scales = {}, {}, {}, {}, {}, {}
         z_biased, y_full, y_rows, a_banks, a_cols = {}, {}, {}, {}, {}
 
         def turn(halves):
@@ -120,16 +122,26 @@ def tile_image_projection_for_similarity_h1_kernel(
                 nc.tensor.transpose(bank[:, slot * P : (slot + 1) * P], half, ident[:])
             return bank
 
+        def sort_x(i, copy, groups):
+            for g in groups:
+                x_sorted[i, g] = work.tile([P, G], BF16, name="x_sorted", bufs=6, align_bytes=256)
+                copy(
+                    out=x_sorted[i, g][:].bitcast(F32).rearrange("m (u q) -> m u q", u=2),
+                    in_=x_rows[i][:].bitcast(F32)[:, 256 * g : 256 * (g + 1)].rearrange("m (q u) -> m u q", u=2),
+                )
+
         def x_halves(i, groups):
+            if (i, 0) in x_sorted:
+                return sorted_halves([x_sorted[i, g] for g in groups])
             words = x_rows[i][:].bitcast(F32)
             return [words[:, 256 * g + u : 256 * (g + 1) : 2] for g in groups for u in range(2)]
 
         def sorted_halves(tiles):
             return [t[:].bitcast(F32)[:, u * P : (u + 1) * P] for t in tiles for u in range(2)]
 
-        def join_halves(bank, count):
-            cols = work.tile([P, 2 * G], BF16, name="cols", align_bytes=64)
-            nc.scalar.copy(
+        def join_halves(bank, count, copy=nc.scalar.copy):
+            cols = work.tile([P, 2 * G], BF16, name="cols", align_bytes=256)
+            copy(
                 out=cols[:, 0 : count * G].bitcast(F32).rearrange("p (g m u) -> p g m u", g=count, u=2),
                 in_=bank[:, 0 : count * 2 * P].rearrange("p (g u m) -> p g m u", g=count, u=2),
             )
@@ -139,8 +151,8 @@ def tile_image_projection_for_similarity_h1_kernel(
             return [(groups, turn(x_halves(i, groups))) for groups in runs]
 
         def quantize_x(i, turned):
-            x_codes[i] = work.tile([P, D_GROUPS, P], U32, name="x_codes", bufs=2, align_bytes=64)
-            x_scales[i] = work.tile([P, D_GROUPS, P], U8, name="x_scales", bufs=2, align_bytes=64)
+            x_codes[i] = work.tile([P, D_GROUPS, P], U32, name="x_codes", bufs=2, align_bytes=256)
+            x_scales[i] = work.tile([P, D_GROUPS, P], U8, name="x_scales", bufs=2, align_bytes=256)
             for groups, bank in turned:
                 cols = join_halves(bank, len(groups))
                 for slot, g in enumerate(groups):
@@ -150,23 +162,26 @@ def tile_image_projection_for_similarity_h1_kernel(
                         in_=cols[:, slot * G : (slot + 1) * G],
                     )
 
+        def hidden_pass(i, c, g, bank):
+            w_scale = wh_scale_first[:, 0, :] if g == 0 else wh_scale_rest[:, g - 1, :]
+            nc.tensor.matmul_mx(
+                out=bank[:],
+                lhsT=x_codes[i][:, g, :].bitcast(FP8X4),
+                lhsT_scale=x_scales[i][:, g, :],
+                rhs=wh[g][:, 2 * c * G : 2 * (c + 1) * G].bitcast(FP4X4),
+                rhs_scale=w_scale[:, c * G : (c + 1) * G],
+                start=(g == 0),
+                stop=(g == D_GROUPS - 1),
+            )
+
         def hidden(i, c):
             bank = next_bank()
             for g in range(D_GROUPS):
-                if c == 0:
-                    w_scale = wh_scale_first[:, g, :]
-                else:
-                    w_scale = wh_scale_rest[:, g, (c - 1) * G : c * G]
-                nc.tensor.matmul_mx(
-                    out=bank[:],
-                    lhsT=x_codes[i][:, g, :].bitcast(FP8X4),
-                    lhsT_scale=x_scales[i][:, g, :],
-                    rhs=wh[c][:, g, :].bitcast(FP4X4),
-                    rhs_scale=w_scale,
-                    start=(g == 0),
-                    stop=(g == D_GROUPS - 1),
-                )
-            a_rows[i, c] = work.tile([P, G], BF16, name="a_rows", bufs=8, align_bytes=64)
+                hidden_pass(i, c, g, bank)
+            add_hidden_bias(i, c, bank)
+
+        def add_hidden_bias(i, c, bank):
+            a_rows[i, c] = work.tile([P, G], BF16, name="a_rows", bufs=8, align_bytes=256)
             nc.vector.tensor_tensor(
                 out=a_rows[i, c][:].rearrange("m (u q j) -> m u q j", u=2, j=2),
                 in0=bank[:].rearrange("m (q u j) -> m u q j", u=2, j=2),
@@ -174,14 +189,16 @@ def tile_image_projection_for_similarity_h1_kernel(
                 op=ALU.add,
             )
 
-        def turn_a(i):
-            for pair in range(H_GROUPS // 2):
-                a_banks[i, pair] = turn(sorted_halves([a_rows[i, 2 * pair], a_rows[i, 2 * pair + 1]]))
+        def turn_a(i, runs):
+            for groups in runs:
+                bank = turn(sorted_halves([a_rows[i, g] for g in groups]))
+                for slot, g in enumerate(groups):
+                    a_banks[i, g] = bank[:].bitcast(BF16)[:, slot * G : (slot + 1) * G]
 
         def relu_a(i):
             for g in range(H_GROUPS):
-                a_cols[i, g] = work.tile([P, G], BF16, name="a_cols", bufs=8, align_bytes=64)
-                pairs = a_banks[i, g // 2][:].bitcast(BF16)[:, (g % 2) * G : (g % 2 + 1) * G]
+                a_cols[i, g] = work.tile([P, G], BF16, name="a_cols", bufs=8, align_bytes=256)
+                pairs = a_banks[i, g]
                 nc.scalar.activation(
                     out=a_cols[i, g][:].rearrange("p (m u j) -> p m u j", u=2, j=2),
                     in_=pairs.rearrange("p (u m j) -> p m u j", u=2, j=2),
@@ -189,52 +206,48 @@ def tile_image_projection_for_similarity_h1_kernel(
                 )
 
         def quantize_a(i, g):
-            a_codes[i, g] = work.tile([P, P], U32, name="a_codes", bufs=8, align_bytes=64)
-            a_scales[i, g] = work.tile([P, P], U8, name="a_scales", bufs=8, align_bytes=64)
+            a_codes[i, g] = work.tile([P, P], U32, name="a_codes", bufs=8, align_bytes=256)
+            a_scales[i, g] = work.tile([P, P], U8, name="a_scales", bufs=8, align_bytes=256)
             nc.vector.quantize_mx(out=a_codes[i, g][:].bitcast(FP8X4), scales=a_scales[i, g][:], in_=a_cols[i, g][:])
 
-        def project(i, e, first=0, width=G):
+        def project(i, e):
             bank = next_bank()
             for g in range(H_GROUPS):
                 nc.tensor.matmul_mx(
-                    out=bank[:, 0:width],
+                    out=bank[:],
                     lhsT=a_codes[i, g][:].bitcast(FP8X4),
                     lhsT_scale=a_scales[i, g][:],
-                    rhs=wp[e][:, g, 2 * first : 2 * (first + width)].bitcast(FP4X4),
-                    rhs_scale=wp_scale[:, g, e * G + first : e * G + first + width],
+                    rhs=wp[g // 2][:, g % 2, 2 * e * G : 2 * (e + 1) * G].bitcast(FP4X4),
+                    rhs_scale=wp_scale[:, g, e * G : (e + 1) * G],
                     start=(g == 0),
                     stop=(g == H_GROUPS - 1),
                 )
             return bank
 
-        def add_proj_bias(i, e, bank, first=0, width=G):
-            if first == 0:
-                z_biased[i, e] = work.tile([P, G], F32, name="z_biased")
+        def add_proj_bias(i, e, bank):
+            z_biased[i, e] = work.tile([P, G], F32, name="z_biased")
             nc.vector.tensor_tensor(
-                out=z_biased[i, e][:, first : first + width],
-                in0=bank[:, 0:width],
-                in1=bp_all[:, e * G + first : e * G + first + width],
-                op=ALU.add,
+                out=z_biased[i, e][:], in0=bank[:], in1=bp_all[:, e * G : (e + 1) * G], op=ALU.add
             )
 
-        def weigh(i, e, first=0, width=G):
-            if first == 0:
-                y_full[i, e] = work.tile([P, G], F32, name="y", bufs=6)
-                y_rows[i, e] = work.tile([P, G], BF16, name="y_rows", bufs=6, align_bytes=64)
-            y = y_full[i, e][:, first : first + width]
+        def weigh(i, e):
+            y = work.tile([P, G], F32, name="y", bufs=6)
+            y_full[i, e] = y
             nc.vector.scalar_tensor_tensor(
-                out=y,
-                in0=z_biased[i, e][:, first : first + width],
+                out=y[:],
+                in0=z_biased[i, e][:],
                 scalar=iw_col[:, i : i + 1],
-                in1=dw_all[:, e * G + first : e * G + first + width],
+                in1=dw_all[:, e * G : (e + 1) * G],
                 op0=ALU.mult,
                 op1=ALU.mult,
             )
-            if first + width == G:
-                nc.sync.dma_start(out=out_0[i * P : (i + 1) * P, e * G : (e + 1) * G], in_=y_full[i, e][:])
-            nc.scalar.copy(
-                out=y_rows[i, e][:].rearrange("m (u q j) -> m u q j", u=2, j=2)[:, :, first // 4 : (first + width) // 4, :],
-                in_=y.rearrange("m (q u j) -> m u q j", u=2, j=2),
+            nc.sync.dma_start(out=out_0[i * P : (i + 1) * P, e * G : (e + 1) * G], in_=y[:])
+
+        def round_y(i, e, copy=nc.scalar.copy):
+            y_rows[i, e] = work.tile([P, G], BF16, name="y_rows", bufs=6, align_bytes=256)
+            copy(
+                out=y_rows[i, e][:].rearrange("m (u q j) -> m u q j", u=2, j=2),
+                in_=y_full[i, e][:].rearrange("m (q u j) -> m u q j", u=2, j=2),
             )
 
         def turn_y(i, groups):
@@ -244,7 +257,7 @@ def tile_image_projection_for_similarity_h1_kernel(
 
         def quantize_y(i, groups, cols):
             for slot, e in enumerate(groups):
-                codes = work.tile([P, P], U32, name="y_codes", bufs=6, align_bytes=64)
+                codes = work.tile([P, P], U32, name="y_codes", bufs=6, align_bytes=256)
                 nc.vector.quantize_mx(
                     out=codes[:].bitcast(FP8X4),
                     scales=y_scales[:, e, i * P : (i + 1) * P],
@@ -252,87 +265,112 @@ def tile_image_projection_for_similarity_h1_kernel(
                 )
                 nc.sync.dma_start(out=out_words[e, :, i * P : (i + 1) * P], in_=codes[:].bitcast(I32))
 
+        def spread_out(bank, dst):
+            nc.scalar.copy(
+                out=dst[:].bitcast(F32).rearrange("p (j c) -> p j c", c=4),
+                in_=bank[:].rearrange("p (c j) -> p j c", c=4),
+            )
+
         for u in range(2):
             bank = spread(bh_cols, [2 * a + u for a in range(4)])
-            nc.vector.tensor_copy(
+            copy = nc.scalar.copy if u == 0 else nc.vector.tensor_copy
+            if u == 1:
+                sort_x(0, nc.vector.tensor_copy, range(D_GROUPS))
+            copy(
                 out=bh_all[:].bitcast(F32).rearrange("p (c u jj a) -> p u c jj a", c=H_GROUPS, u=2, a=4)[:, u],
                 in_=bank[:].rearrange("p (a c jj) -> p c jj a", a=4, c=H_GROUPS),
             )
         quantize_x(0, turn_x(0, [[g] for g in range(D_GROUPS)]))
+        first_banks = [next_bank() for c in range(H_GROUPS)]
+        for g in range(D_GROUPS):
+            for c in range(H_GROUPS):
+                hidden_pass(0, c, g, first_banks[c])
+        for c in range(H_GROUPS):
+            add_hidden_bias(0, c, first_banks[c])
+        x_turned = turn_x(1, [[0, 1], [2]])
+        bp_bank = spread(bp_cols, range(4))
+        quantize_x(1, x_turned)
+        turn_a(0, [[0, 1], [2, 3]])
+        spread_out(bp_bank, bp_all)
+        sort_x(2, nc.scalar.copy, range(D_GROUPS))
+        relu_a(0)
+        nc.vector.tensor_copy(out=iw_rows32[:], in_=iw_rows[:])
 
         both = list(range(E_GROUPS))
         last = TILES - 1
-        for i in range(TILES):
+        for i in range(1, TILES):
             if i == last:
                 early_bank = project(i - 1, 0)
-                weigh(i - 2, 1)
                 add_proj_bias(i - 1, 0, early_bank)
+            elif i > 1:
+                sort_x(i + 1, nc.scalar.copy, range(D_GROUPS))
             for c in range(H_GROUPS):
                 hidden(i, c)
+                if i == 1:
+                    quantize_a(0, c)
                 if c == 0 and i >= 2:
-                    if i == last:
-                        weigh(i - 1, 0)
-                    else:
-                        weigh(i - 2, 1)
-                if c == 1 and i == 0:
-                    quantize_x(1, turn_x(1, [[0, 1], [2]]))
-            if i == 0:
-                nc.vector.tensor_copy(out=iw_rows32[:], in_=iw_rows[:])
-                spread_banks = [spread(cols, range(4)) for cols in (bp_cols, dw_cols)]
+                    weigh(i - 2, 1)
+                    round_y(i - 2, 1)
+            if i == last:
+                break
+            x_turned = turn_x(i + 1, [[0, 1], [2]])
+            if i == 1:
+                dw_bank = spread(dw_cols, range(4))
                 iw_bank = turn([iw_rows32[:]])
-                turn_a(i)
-                relu_a(i)
-                for bank, dst in zip(spread_banks, (bp_all, dw_all)):
-                    nc.scalar.copy(
-                        out=dst[:].bitcast(F32).rearrange("p (j c) -> p j c", c=4),
-                        in_=bank[:].rearrange("p (c j) -> p j c", c=4),
-                    )
+            else:
+                y_bank = turn_y(i - 2, both)
+            turn_a(i, [[0, 1], [2, 3]])
+            quantize_x(i + 1, x_turned)
+            if i == 1:
+                spread_out(dw_bank, dw_all)
                 nc.scalar.copy(out=iw_col[:], in_=iw_bank[:, 0:TILES])
-                for g in range(H_GROUPS):
-                    quantize_a(i, g)
-                continue
-            x_turned = turn_x(i + 1, [[0, 1], [2]]) if i < last else []
-            y_bank = turn_y(i - 2, both) if i >= 2 else None
-            turn_a(i)
-            if i < last:
-                quantize_x(i + 1, x_turned)
             relu_a(i)
             y_cols = join_halves(y_bank, E_GROUPS) if i >= 2 else None
             quantize_a(i, 0)
-            if i < last:
-                add_proj_bias(i - 1, 0, project(i - 1, 0))
-                quantize_a(i, 1)
-                weigh(i - 1, 0)
-                quantize_a(i, 2)
-                quantize_a(i, 3)
-                if i >= 2:
-                    quantize_y(i - 2, both, y_cols)
-                add_proj_bias(i - 1, 1, project(i - 1, 1))
+            add_proj_bias(i - 1, 0, project(i - 1, 0))
+            quantize_a(i, 1)
+            quantize_a(i, 2)
+            weigh(i - 1, 0)
+            round_y(i - 1, 0)
+            quantize_a(i, 3)
+            if i >= 2:
+                quantize_y(i - 2, both, y_cols)
+            add_proj_bias(i - 1, 1, project(i - 1, 1))
 
+        def store_scales(first, stop, queues):
+            for q in range(4):
+                queues[q % len(queues)].dma_start(
+                    out=out_2.bitcast(I32)[:, 4 * q : 4 * q + 4, first // 4 : stop // 4].rearrange("g r w -> r g w"),
+                    in_=y_scales[32 * q : 32 * q + 4].bitcast(I32)[:, :, first // 4 : stop // 4],
+                )
+
+        turn_a(last, [[0], [1]])
+        y_bank = turn_y(last - 2, both)
+        turn_a(last, [[2], [3]])
+        relu_a(last)
+        weigh(last - 1, 0)
+        round_y(last - 1, 0)
+        quantize_a(last, 0)
+        y_cols = join_halves(y_bank, E_GROUPS, nc.vector.tensor_copy)
         quantize_a(last, 1)
-        add_proj_bias(last - 1, 1, project(last - 1, 1))
         quantize_a(last, 2)
-        quantize_a(last, 3)
-        bank0 = project(last, 0)
-        weigh(last - 1, 1)
-        add_proj_bias(last, 0, bank0)
-        part_banks = [project(last, 1, first, P) for first in range(0, G, P)]
         quantize_y(last - 2, both, y_cols)
-        weigh(last, 0)
+        store_scales(0, (last - 1) * P, [nc.sync])
+        late_bank = project(last - 1, 1)
+        quantize_a(last, 3)
+        add_proj_bias(last - 1, 1, late_bank)
+        bank0 = project(last, 0)
+        bank1 = project(last, 1)
+        weigh(last - 1, 1)
+        round_y(last - 1, 1)
+        add_proj_bias(last, 0, bank0)
+        add_proj_bias(last, 1, bank1)
         before_cols = join_halves(turn_y(last - 1, both), E_GROUPS)
-        for part, bank in enumerate(part_banks):
-            add_proj_bias(last, 1, bank, part * P, P)
-            if part > 0:
-                weigh(last, 1, (part - 1) * P, P)
-        first_cols = join_halves(turn_y(last, [0]), 1)
-        quantize_y(last - 1, [0], before_cols)
-        weigh(last, 1, G - P, P)
-        quantize_y(last - 1, [1], before_cols[:, G : 2 * G])
-        quantize_y(last, [0], first_cols)
-        quantize_y(last, [1], join_halves(turn_y(last, [1]), 1))
-        for q in range(4):
-            queue = nc.scalar if q % 2 == 0 else nc.sync
-            queue.dma_start(
-                out=out_2.bitcast(I32)[:, 4 * q : 4 * q + 4, :].rearrange("g r w -> r g w"),
-                in_=y_scales[32 * q : 32 * q + 4].bitcast(I32),
-            )
+        weigh(last, 0)
+        round_y(last, 0)
+        weigh(last, 1)
+        quantize_y(last - 1, both, before_cols)
+        round_y(last, 1, nc.vector.tensor_copy)
+        for e in both:
+            quantize_y(last, [e], join_halves(turn_y(last, [e]), 1))
+        store_scales((last - 1) * P, M, [nc.scalar, nc.sync])

@@ -60,7 +60,7 @@ def tile_image_projection_for_similarity_h1_kernel(
         bp_all = kept("bp_all", [P, E], BF16)
         dw_all = kept("dw_all", [P, E], BF16)
         iw_col = kept("iw_col", [P, TILES], F32)
-        y_scales = kept("y_scales", [P, E_GROUPS, M], U8)
+        y_scales = [kept("y_scales%d" % half, [P, E_GROUPS, M // 2], U8) for half in range(2)]
 
         nc.vector.memset(wh_scale_first[:].bitcast(I32), 0)
         nc.vector.memset(wh_scale_rest[:].bitcast(I32), 0)
@@ -140,7 +140,7 @@ def tile_image_projection_for_similarity_h1_kernel(
             return [t[:].bitcast(F32)[:, u * P : (u + 1) * P] for t in tiles for u in range(2)]
 
         def join_halves(bank, count, copy=nc.scalar.copy):
-            cols = work.tile([P, 2 * G], BF16, name="cols", align_bytes=256)
+            cols = work.tile([P, 2 * G], BF16, name="cols", bufs=6, align_bytes=256)
             copy(
                 out=cols[:, 0 : count * G].bitcast(F32).rearrange("p (g m u) -> p g m u", g=count, u=2),
                 in_=bank[:, 0 : count * 2 * P].rearrange("p (g u m) -> p g m u", g=count, u=2),
@@ -250,17 +250,17 @@ def tile_image_projection_for_similarity_h1_kernel(
                 in_=y_full[i, e][:].rearrange("m (q u j) -> m u q j", u=2, j=2),
             )
 
-        def turn_y(i, groups):
-            return turn(sorted_halves([y_rows[i, e] for e in groups]))
+        def turn_y(chunks):
+            return turn(sorted_halves([y_rows[chunk] for chunk in chunks]))
 
         out_words = out_1.rearrange("g p m t -> g p (m t)").bitcast(I32)
 
-        def quantize_y(i, groups, cols):
-            for slot, e in enumerate(groups):
-                codes = work.tile([P, P], U32, name="y_codes", bufs=6, align_bytes=256)
+        def quantize_y(chunks, cols):
+            for slot, (i, e) in enumerate(chunks):
+                codes = work.tile([P, P], U32, name="y_codes", bufs=12, align_bytes=256)
                 nc.vector.quantize_mx(
                     out=codes[:].bitcast(FP8X4),
-                    scales=y_scales[:, e, i * P : (i + 1) * P],
+                    scales=y_scales[i // 3][:, e, (i % 3) * P : (i % 3 + 1) * P],
                     in_=cols[:, slot * G : (slot + 1) * G],
                 )
                 nc.sync.dma_start(out=out_words[e, :, i * P : (i + 1) * P], in_=codes[:].bitcast(I32))
@@ -296,36 +296,46 @@ def tile_image_projection_for_similarity_h1_kernel(
         relu_a(0)
         nc.vector.tensor_copy(out=iw_rows32[:], in_=iw_rows[:])
 
-        both = list(range(E_GROUPS))
         last = TILES - 1
-        for i in range(1, TILES):
-            if i == last:
-                early_bank = project(i - 1, 0)
-                add_proj_bias(i - 1, 0, early_bank)
-            elif i > 1:
-                sort_x(i + 1, nc.scalar.copy, range(D_GROUPS))
+
+        def store_scales(half, queues):
+            words = M // 2 // 4
+            for q in range(4):
+                dst = out_2.bitcast(I32)[:, 4 * q : 4 * q + 4, half * words : (half + 1) * words]
+                queues[q % len(queues)].dma_start(
+                    out=dst.rearrange("g r w -> r g w"),
+                    in_=y_scales[half][32 * q : 32 * q + 4].bitcast(I32),
+                )
+
+        waiting = []
+        for i in range(1, last):
             for c in range(H_GROUPS):
                 hidden(i, c)
                 if i == 1:
                     quantize_a(0, c)
-                if c == 0 and i >= 2:
-                    weigh(i - 2, 1)
-                    round_y(i - 2, 1)
-            if i == last:
-                break
+                if c == 1 and waiting:
+                    quantize_y(*waiting.pop())
             x_turned = turn_x(i + 1, [[0, 1], [2]])
+            chunks = [(t, e) for t, e in ((i - 3, 1), (i - 2, 0)) if t >= 0]
             if i == 1:
                 dw_bank = spread(dw_cols, range(4))
                 iw_bank = turn([iw_rows32[:]])
             else:
-                y_bank = turn_y(i - 2, both)
+                y_bank = turn_y(chunks)
             turn_a(i, [[0, 1], [2, 3]])
+            if i >= 2:
+                weigh(i - 2, 1)
             quantize_x(i + 1, x_turned)
+            if i >= 2:
+                round_y(i - 2, 1, nc.vector.tensor_copy)
             if i == 1:
                 spread_out(dw_bank, dw_all)
                 nc.scalar.copy(out=iw_col[:], in_=iw_bank[:, 0:TILES])
             relu_a(i)
-            y_cols = join_halves(y_bank, E_GROUPS) if i >= 2 else None
+            if i >= 2:
+                waiting.append((chunks, join_halves(y_bank, len(chunks))))
+            if i + 2 <= last:
+                sort_x(i + 2, nc.scalar.copy, range(D_GROUPS))
             quantize_a(i, 0)
             add_proj_bias(i - 1, 0, project(i - 1, 0))
             quantize_a(i, 1)
@@ -333,44 +343,48 @@ def tile_image_projection_for_similarity_h1_kernel(
             weigh(i - 1, 0)
             round_y(i - 1, 0)
             quantize_a(i, 3)
-            if i >= 2:
-                quantize_y(i - 2, both, y_cols)
             add_proj_bias(i - 1, 1, project(i - 1, 1))
 
-        def store_scales(first, stop, queues):
-            for q in range(4):
-                queues[q % len(queues)].dma_start(
-                    out=out_2.bitcast(I32)[:, 4 * q : 4 * q + 4, first // 4 : stop // 4].rearrange("g r w -> r g w"),
-                    in_=y_scales[32 * q : 32 * q + 4].bitcast(I32)[:, :, first // 4 : stop // 4],
-                )
-
+        quantize_y(*waiting.pop())
+        for c in range(H_GROUPS):
+            hidden(last, c)
+            if c == 0:
+                weigh(last - 2, 1)
+                round_y(last - 2, 1)
+                add_proj_bias(last - 1, 0, project(last - 1, 0))
         turn_a(last, [[0], [1]])
-        y_bank = turn_y(last - 2, both)
+        early = [(last - 3, 1), (last - 2, 0)]
+        early_bank = turn_y(early)
+        late = [(last - 2, 1)]
+        late_y_bank = turn_y(late)
         turn_a(last, [[2], [3]])
         relu_a(last)
         weigh(last - 1, 0)
+        late_cols = join_halves(late_y_bank, 1)
         round_y(last - 1, 0)
         quantize_a(last, 0)
-        y_cols = join_halves(y_bank, E_GROUPS, nc.vector.tensor_copy)
+        early_cols = join_halves(early_bank, 2, nc.vector.tensor_copy)
         quantize_a(last, 1)
         quantize_a(last, 2)
-        quantize_y(last - 2, both, y_cols)
-        store_scales(0, (last - 1) * P, [nc.sync])
+        quantize_y(early, early_cols)
+        store_scales(0, [nc.sync])
         late_bank = project(last - 1, 1)
         quantize_a(last, 3)
         add_proj_bias(last - 1, 1, late_bank)
+        quantize_y(late, late_cols)
         bank0 = project(last, 0)
         bank1 = project(last, 1)
         weigh(last - 1, 1)
         round_y(last - 1, 1)
         add_proj_bias(last, 0, bank0)
         add_proj_bias(last, 1, bank1)
-        before_cols = join_halves(turn_y(last - 1, both), E_GROUPS)
+        before = [(last - 1, 0), (last - 1, 1)]
+        before_cols = join_halves(turn_y(before), 2)
         weigh(last, 0)
         round_y(last, 0)
         weigh(last, 1)
-        quantize_y(last - 1, both, before_cols)
+        quantize_y(before, before_cols)
         round_y(last, 1, nc.vector.tensor_copy)
-        for e in both:
-            quantize_y(last, [e], join_halves(turn_y(last, [e]), 1))
-        store_scales((last - 1) * P, M, [nc.scalar, nc.sync])
+        for e in range(E_GROUPS):
+            quantize_y([(last, e)], join_halves(turn_y([(last, e)]), 1))
+        store_scales(1, [nc.scalar, nc.sync])

from contextlib import ExitStack

import concourse.mybir as mybir
from concourse.masks import make_identity

M, D, H, E = 768, 1536, 2048, 1024
FLOPS = 2 * M * (D * H + H * E)

F32 = mybir.dt.float32
BF16 = mybir.dt.bfloat16
I32 = mybir.dt.int32
U32 = mybir.dt.uint32
U8 = mybir.dt.uint8
FP8X4 = mybir.dt.float8_e4m3fn_x4
FP4X4 = mybir.dt.float4_e2m1fn_x4
ALU = mybir.AluOpType
ACT = mybir.ActivationFunctionType

P = 128
G = 512
TILES = M // P
D_GROUPS, H_GROUPS, E_GROUPS = D // G, H // G, E // G
BANKS = 8


def tile_image_projection_for_similarity_h1_kernel(
    tc, pooled, hidden_words, hidden_scales, b_hidden, proj_words, proj_scales, b_proj, dim_weight, image_weight,
    out_0, out_1, out_2,
):
    nc = tc.nc
    with ExitStack() as ctx:
        keep = ctx.enter_context(tc.tile_pool(name="keep", bufs=1))
        work = ctx.enter_context(tc.tile_pool(name="work", bufs=4))
        psum = ctx.enter_context(tc.psum_pool(name="psum", bufs=1))
        ctx.enter_context(tc.manual_schedule())

        banks_taken = []

        def next_bank():
            n = len(banks_taken) % BANKS
            banks_taken.append(n)
            return psum.tile([P, G], F32, name="bank%d" % n)

        def kept(name, shape, dtype):
            return keep.tile(shape, dtype, name=name, align_bytes=256)

        ident = kept("ident", [P, P], F32)
        x_rows = [kept("x_rows%d" % i, [P, D], BF16) for i in range(TILES)]
        wh = [kept("wh%d" % g, [P, 2 * H], U8) for g in range(D_GROUPS)]
        wp = [kept("wp%d" % half, [P, 2, 2 * E], U8) for half in range(H_GROUPS // 2)]
        wh_scale_first = kept("wh_scale_first", [P, 1, H], U8)
        wh_scale_rest = kept("wh_scale_rest", [P, D_GROUPS - 1, H], U8)
        wp_scale = kept("wp_scale", [P, H_GROUPS, E], U8)
        bh_cols = kept("bh_cols", [P, H // P], BF16)
        bp_cols = kept("bp_cols", [P, E // P], BF16)
        dw_cols = kept("dw_cols", [P, E // P], BF16)
        iw_rows = kept("iw_rows", [P, P], BF16)
        iw_rows32 = kept("iw_rows32", [P, P], F32)
        bh_all = kept("bh_all", [P, H], BF16)
        bp_all = kept("bp_all", [P, E], BF16)
        dw_all = kept("dw_all", [P, E], BF16)
        iw_col = kept("iw_col", [P, TILES], F32)
        y_scales = [kept("y_scales%d" % half, [P, E_GROUPS, M // 2], U8) for half in range(2)]

        nc.vector.memset(wh_scale_first[:].bitcast(I32), 0)
        nc.vector.memset(wh_scale_rest[:].bitcast(I32), 0)
        make_identity(nc, ident[:])
        nc.scalar.activation(out=iw_rows[:], in_=ident[:], func=ACT.Copy, scale=0.0)
        nc.gpsimd.memset(wp_scale[:].bitcast(I32), 0)

        def load_x(i):
            nc.sync.dma_start(out=x_rows[i][:], in_=pooled[i * P : (i + 1) * P, :])

        def load_wh(g):
            nc.sync.dma_start(out=wh[g][:].bitcast(I32), in_=hidden_words.bitcast(I32)[g])

        def load_wp(half):
            src = proj_words.bitcast(I32)[2 * half : 2 * half + 2]
            nc.sync.dma_start(out=wp[half][:].bitcast(I32), in_=src.rearrange("g p w -> p g w"))

        def load_scales(tile, scales, first, last):
            for q in range(4):
                src = scales.bitcast(I32)[first:last, 4 * q : 4 * q + 4, :]
                nc.sync.dma_start(out=tile[32 * q : 32 * q + 4].bitcast(I32), in_=src.rearrange("g r w -> r g w"))

        def load_cols(tile, vec):
            nc.sync.dma_start(out=tile[:], in_=vec.rearrange("(p c) -> p c", p=P))

        load_cols(bh_cols, b_hidden)
        load_x(0)
        load_scales(wh_scale_first, hidden_scales, 0, 1)
        load_wh(0)
        load_scales(wh_scale_rest, hidden_scales, 1, D_GROUPS)
        load_wh(1)
        load_wh(2)
        load_x(1)
        load_cols(bp_cols, b_proj)
        load_x(2)
        load_cols(dw_cols, dim_weight)
        nc.sync.dma_start(out=iw_rows[0:TILES, :], in_=image_weight.rearrange("(i m) -> i m", m=P))
        load_scales(wp_scale, proj_scales, 0, H_GROUPS)
        load_wp(0)
        load_wp(1)
        for i in range(3, TILES):
            load_x(i)

        def spread(cols, picks):
            bank = next_bank()
            words = cols[:].bitcast(F32)
            for slot, c in enumerate(picks):
                nc.tensor.transpose(
                    bank[:, slot * P : (slot + 1) * P], words[:, c : c + 1].to_broadcast([P, P]), ident[:]
                )
            return bank

        x_sorted, x_codes, x_scales, a_rows, a_codes, a_scales = {}, {}, {}, {}, {}, {}
        z_biased, y_full, y_rows, a_banks, a_cols = {}, {}, {}, {}, {}

        def turn(halves):
            bank = next_bank()
            for slot, half in enumerate(halves):
                nc.tensor.transpose(bank[:, slot * P : (slot + 1) * P], half, ident[:])
            return bank

        def sort_x(i, copy, groups):
            for g in groups:
                x_sorted[i, g] = work.tile([P, G], BF16, name="x_sorted", bufs=6, align_bytes=256)
                copy(
                    out=x_sorted[i, g][:].bitcast(F32).rearrange("m (u q) -> m u q", u=2),
                    in_=x_rows[i][:].bitcast(F32)[:, 256 * g : 256 * (g + 1)].rearrange("m (q u) -> m u q", u=2),
                )

        def x_halves(i, groups):
            if (i, 0) in x_sorted:
                return sorted_halves([x_sorted[i, g] for g in groups])
            words = x_rows[i][:].bitcast(F32)
            return [words[:, 256 * g + u : 256 * (g + 1) : 2] for g in groups for u in range(2)]

        def sorted_halves(tiles):
            return [t[:].bitcast(F32)[:, u * P : (u + 1) * P] for t in tiles for u in range(2)]

        def join_halves(bank, count, copy=nc.scalar.copy):
            cols = work.tile([P, 2 * G], BF16, name="cols", bufs=6, align_bytes=256)
            copy(
                out=cols[:, 0 : count * G].bitcast(F32).rearrange("p (g m u) -> p g m u", g=count, u=2),
                in_=bank[:, 0 : count * 2 * P].rearrange("p (g u m) -> p g m u", g=count, u=2),
            )
            return cols

        def turn_x(i, runs):
            return [(groups, turn(x_halves(i, groups))) for groups in runs]

        def quantize_x(i, turned):
            x_codes[i] = work.tile([P, D_GROUPS, P], U32, name="x_codes", bufs=2, align_bytes=256)
            x_scales[i] = work.tile([P, D_GROUPS, P], U8, name="x_scales", bufs=2, align_bytes=256)
            for groups, bank in turned:
                cols = join_halves(bank, len(groups))
                for slot, g in enumerate(groups):
                    nc.vector.quantize_mx(
                        out=x_codes[i][:, g, :].bitcast(FP8X4),
                        scales=x_scales[i][:, g, :],
                        in_=cols[:, slot * G : (slot + 1) * G],
                    )

        def hidden_pass(i, c, g, bank):
            w_scale = wh_scale_first[:, 0, :] if g == 0 else wh_scale_rest[:, g - 1, :]
            nc.tensor.matmul_mx(
                out=bank[:],
                lhsT=x_codes[i][:, g, :].bitcast(FP8X4),
                lhsT_scale=x_scales[i][:, g, :],
                rhs=wh[g][:, 2 * c * G : 2 * (c + 1) * G].bitcast(FP4X4),
                rhs_scale=w_scale[:, c * G : (c + 1) * G],
                start=(g == 0),
                stop=(g == D_GROUPS - 1),
            )

        def hidden(i, c):
            bank = next_bank()
            for g in range(D_GROUPS):
                hidden_pass(i, c, g, bank)
            add_hidden_bias(i, c, bank)

        def add_hidden_bias(i, c, bank):
            a_rows[i, c] = work.tile([P, G], BF16, name="a_rows", bufs=8, align_bytes=256)
            nc.vector.tensor_tensor(
                out=a_rows[i, c][:].rearrange("m (u q j) -> m u q j", u=2, j=2),
                in0=bank[:].rearrange("m (q u j) -> m u q j", u=2, j=2),
                in1=bh_all[:, c * G : (c + 1) * G].rearrange("m (u q j) -> m u q j", u=2, j=2),
                op=ALU.add,
            )

        def turn_a(i, runs):
            for groups in runs:
                bank = turn(sorted_halves([a_rows[i, g] for g in groups]))
                for slot, g in enumerate(groups):
                    a_banks[i, g] = bank[:].bitcast(BF16)[:, slot * G : (slot + 1) * G]

        def relu_a(i):
            for g in range(H_GROUPS):
                a_cols[i, g] = work.tile([P, G], BF16, name="a_cols", bufs=8, align_bytes=256)
                pairs = a_banks[i, g]
                nc.scalar.activation(
                    out=a_cols[i, g][:].rearrange("p (m u j) -> p m u j", u=2, j=2),
                    in_=pairs.rearrange("p (u m j) -> p m u j", u=2, j=2),
                    func=ACT.Relu,
                )

        def quantize_a(i, g):
            a_codes[i, g] = work.tile([P, P], U32, name="a_codes", bufs=8, align_bytes=256)
            a_scales[i, g] = work.tile([P, P], U8, name="a_scales", bufs=8, align_bytes=256)
            nc.vector.quantize_mx(out=a_codes[i, g][:].bitcast(FP8X4), scales=a_scales[i, g][:], in_=a_cols[i, g][:])

        def project(i, e):
            bank = next_bank()
            for g in range(H_GROUPS):
                nc.tensor.matmul_mx(
                    out=bank[:],
                    lhsT=a_codes[i, g][:].bitcast(FP8X4),
                    lhsT_scale=a_scales[i, g][:],
                    rhs=wp[g // 2][:, g % 2, 2 * e * G : 2 * (e + 1) * G].bitcast(FP4X4),
                    rhs_scale=wp_scale[:, g, e * G : (e + 1) * G],
                    start=(g == 0),
                    stop=(g == H_GROUPS - 1),
                )
            return bank

        def add_proj_bias(i, e, bank):
            z_biased[i, e] = work.tile([P, G], F32, name="z_biased")
            nc.vector.tensor_tensor(
                out=z_biased[i, e][:], in0=bank[:], in1=bp_all[:, e * G : (e + 1) * G], op=ALU.add
            )

        def weigh(i, e):
            y = work.tile([P, G], F32, name="y", bufs=6)
            y_full[i, e] = y
            nc.vector.scalar_tensor_tensor(
                out=y[:],
                in0=z_biased[i, e][:],
                scalar=iw_col[:, i : i + 1],
                in1=dw_all[:, e * G : (e + 1) * G],
                op0=ALU.mult,
                op1=ALU.mult,
            )
            nc.sync.dma_start(out=out_0[i * P : (i + 1) * P, e * G : (e + 1) * G], in_=y[:])

        def round_y(i, e, copy=nc.scalar.copy):
            y_rows[i, e] = work.tile([P, G], BF16, name="y_rows", bufs=6, align_bytes=256)
            copy(
                out=y_rows[i, e][:].rearrange("m (u q j) -> m u q j", u=2, j=2),
                in_=y_full[i, e][:].rearrange("m (q u j) -> m u q j", u=2, j=2),
            )

        def turn_y(chunks):
            return turn(sorted_halves([y_rows[chunk] for chunk in chunks]))

        out_words = out_1.rearrange("g p m t -> g p (m t)").bitcast(I32)

        def quantize_y(chunks, cols):
            for slot, (i, e) in enumerate(chunks):
                codes = work.tile([P, P], U32, name="y_codes", bufs=12, align_bytes=256)
                nc.vector.quantize_mx(
                    out=codes[:].bitcast(FP8X4),
                    scales=y_scales[i // 3][:, e, (i % 3) * P : (i % 3 + 1) * P],
                    in_=cols[:, slot * G : (slot + 1) * G],
                )
                nc.sync.dma_start(out=out_words[e, :, i * P : (i + 1) * P], in_=codes[:].bitcast(I32))

        def spread_out(bank, dst):
            nc.scalar.copy(
                out=dst[:].bitcast(F32).rearrange("p (j c) -> p j c", c=4),
                in_=bank[:].rearrange("p (c j) -> p j c", c=4),
            )

        for u in range(2):
            bank = spread(bh_cols, [2 * a + u for a in range(4)])
            copy = nc.scalar.copy if u == 0 else nc.vector.tensor_copy
            if u == 1:
                sort_x(0, nc.vector.tensor_copy, range(D_GROUPS))
            copy(
                out=bh_all[:].bitcast(F32).rearrange("p (c u jj a) -> p u c jj a", c=H_GROUPS, u=2, a=4)[:, u],
                in_=bank[:].rearrange("p (a c jj) -> p c jj a", a=4, c=H_GROUPS),
            )
        quantize_x(0, turn_x(0, [[g] for g in range(D_GROUPS)]))
        first_banks = [next_bank() for c in range(H_GROUPS)]
        for g in range(D_GROUPS):
            for c in range(H_GROUPS):
                hidden_pass(0, c, g, first_banks[c])
        for c in range(H_GROUPS):
            add_hidden_bias(0, c, first_banks[c])
        x_turned = turn_x(1, [[0, 1], [2]])
        bp_bank = spread(bp_cols, range(4))
        quantize_x(1, x_turned)
        turn_a(0, [[0, 1], [2, 3]])
        spread_out(bp_bank, bp_all)
        sort_x(2, nc.scalar.copy, range(D_GROUPS))
        relu_a(0)
        nc.vector.tensor_copy(out=iw_rows32[:], in_=iw_rows[:])

        last = TILES - 1

        def store_scales(half, queues):
            words = M // 2 // 4
            for q in range(4):
                dst = out_2.bitcast(I32)[:, 4 * q : 4 * q + 4, half * words : (half + 1) * words]
                queues[q % len(queues)].dma_start(
                    out=dst.rearrange("g r w -> r g w"),
                    in_=y_scales[half][32 * q : 32 * q + 4].bitcast(I32),
                )

        waiting = []
        for i in range(1, last):
            for c in range(H_GROUPS):
                hidden(i, c)
                if i == 1:
                    quantize_a(0, c)
                if c == 1 and waiting:
                    quantize_y(*waiting.pop())
            x_turned = turn_x(i + 1, [[0, 1], [2]])
            chunks = [(t, e) for t, e in ((i - 3, 1), (i - 2, 0)) if t >= 0]
            if i == 1:
                dw_bank = spread(dw_cols, range(4))
                iw_bank = turn([iw_rows32[:]])
            else:
                y_bank = turn_y(chunks)
            turn_a(i, [[0, 1], [2, 3]])
            if i >= 2:
                weigh(i - 2, 1)
            quantize_x(i + 1, x_turned)
            if i >= 2:
                round_y(i - 2, 1, nc.vector.tensor_copy)
            if i == 1:
                spread_out(dw_bank, dw_all)
                nc.scalar.copy(out=iw_col[:], in_=iw_bank[:, 0:TILES])
            relu_a(i)
            if i >= 2:
                waiting.append((chunks, join_halves(y_bank, len(chunks))))
            if i + 2 <= last:
                sort_x(i + 2, nc.scalar.copy, range(D_GROUPS))
            quantize_a(i, 0)
            add_proj_bias(i - 1, 0, project(i - 1, 0))
            quantize_a(i, 1)
            quantize_a(i, 2)
            weigh(i - 1, 0)
            round_y(i - 1, 0)
            quantize_a(i, 3)
            add_proj_bias(i - 1, 1, project(i - 1, 1))

        quantize_y(*waiting.pop())
        for c in range(H_GROUPS):
            hidden(last, c)
            if c == 0:
                weigh(last - 2, 1)
                round_y(last - 2, 1)
                add_proj_bias(last - 1, 0, project(last - 1, 0))
        turn_a(last, [[0], [1]])
        early = [(last - 3, 1), (last - 2, 0)]
        early_bank = turn_y(early)
        late = [(last - 2, 1)]
        late_y_bank = turn_y(late)
        turn_a(last, [[2], [3]])
        relu_a(last)
        weigh(last - 1, 0)
        late_cols = join_halves(late_y_bank, 1)
        round_y(last - 1, 0)
        quantize_a(last, 0)
        early_cols = join_halves(early_bank, 2, nc.vector.tensor_copy)
        quantize_a(last, 1)
        quantize_a(last, 2)
        quantize_y(early, early_cols)
        store_scales(0, [nc.sync])
        late_bank = project(last - 1, 1)
        quantize_a(last, 3)
        add_proj_bias(last - 1, 1, late_bank)
        quantize_y(late, late_cols)
        bank0 = project(last, 0)
        bank1 = project(last, 1)
        weigh(last - 1, 1)
        round_y(last - 1, 1)
        add_proj_bias(last, 0, bank0)
        add_proj_bias(last, 1, bank1)
        before = [(last - 1, 0), (last - 1, 1)]
        before_cols = join_halves(turn_y(before), 2)
        weigh(last, 0)
        round_y(last, 0)
        weigh(last, 1)
        quantize_y(before, before_cols)
        round_y(last, 1, nc.vector.tensor_copy)
        for e in range(E_GROUPS):
            quantize_y([(last, e)], join_halves(turn_y([(last, e)]), 1))
        store_scales(1, [nc.scalar, nc.sync])
